import numpy as np
CORES = [7,6,5,4,3,2,1,0]
N = 8
H = 8
ROWS, COLS = 2, 4
PERIODIC = True
def setup_inputs(rng):
    return {"x": rng.standard_normal((N, 128, 128), dtype=np.float32)}
def reference(x):
    W = x.shape[2]
    y = np.zeros((N, 4, 128, H), x.dtype)
    for r in range(N):
        i, j = divmod(r, COLS)
        for k, (di, dj, cols) in enumerate([(-1, 0, slice(W - H, W)), (1, 0, slice(0, H)), (0, -1, slice(W - H, W)), (0, 1, slice(0, H))]):
            a, b = i + di, j + dj
            if PERIODIC:
                a, b = a % ROWS, b % COLS
            if 0 <= a < ROWS and 0 <= b < COLS:
                y[r][k] = x[a * COLS + b][:, cols]
    return {"y": y}

@@ -1,0 +1,53 @@
+from concourse.bass import DstId, RemoteDMATransfer
+
+H = 8
+ROWS, COLS = 2, 4
+
+SCRATCH = {
+    "xs": ("sbuf", [128, 128], "float32"),
+    "halo": ("dram", [4, 128, H], "float32"),
+}
+SEMAPHORES = ["loaded", "read", "arrived", "stored"]
+
+LOW, HIGH = 0x00FF, 0xFF00
+NORTH, SOUTH, WEST, EAST = 0, 1, 2, 3
+
+
+def rank_program(g, core, T, topo):
+    rank = T.rank_of(core)
+    if rank is None:
+        return
+    i, j = divmod(rank, COLS)
+    w = T.x.shape[1]
+
+    def dst_id(a, b):
+        rid, pid, sengine = topo.addr(T.cores[(a % ROWS) * COLS + (b % COLS)])
+        return DstId(rid=rid, pnc=pid)
+
+    g.dma_start(T.xs[:], T.x[:]).then_inc(T.sem.loaded, 16)
+    g.wait_ge(T.sem.loaded, 16)
+
+    g.remote_dma_fused(
+        [
+            RemoteDMATransfer(
+                srcs=[T.xs[:, w - H:w]],
+                dsts=[T.halo[NORTH], T.halo[WEST]],
+                dst_ids=[dst_id(i + 1, j), dst_id(i, j + 1)],
+                dma_engine_mask=LOW,
+                remote_sem=T.sem.arrived,
+            ),
+            RemoteDMATransfer(
+                srcs=[T.xs[:, 0:H]],
+                dsts=[T.halo[SOUTH], T.halo[EAST]],
+                dst_ids=[dst_id(i - 1, j), dst_id(i, j - 1)],
+                dma_engine_mask=HIGH,
+                remote_sem=T.sem.arrived,
+            ),
+        ],
+        local_sem=T.sem.read,
+    )
+
+    g.wait_ge(T.sem.arrived, 32)
+    g.dma_start(T.y[:], T.halo[:]).then_inc(T.sem.stored, 16)
+    g.wait_ge(T.sem.stored, 16)
+    g.wait_ge(T.sem.read, 16)

@@ -4,12 +4,13 @@ H = 8
 ROWS, COLS = 2, 4
 
 SCRATCH = {
-    "xs": ("sbuf", [128, 128], "float32"),
+    "edge": ("dram", [2, 128, H], "float32"),
     "halo": ("dram", [4, 128, H], "float32"),
 }
 SEMAPHORES = ["loaded", "read", "arrived", "stored"]
 
 LOW, HIGH = 0x00FF, 0xFF00
+LAST, FIRST = 0, 1
 NORTH, SOUTH, WEST, EAST = 0, 1, 2, 3
 
 
@@ -24,20 +25,21 @@ def rank_program(g, core, T, topo):
         rid, pid, sengine = topo.addr(T.cores[(a % ROWS) * COLS + (b % COLS)])
         return DstId(rid=rid, pnc=pid)
 
-    g.dma_start(T.xs[:], T.x[:]).then_inc(T.sem.loaded, 16)
-    g.wait_ge(T.sem.loaded, 16)
+    g.dma_start(T.edge[LAST], T.x[:, w - H:w]).then_inc(T.sem.loaded, 16)
+    g.dma_start(T.edge[FIRST], T.x[:, 0:H]).then_inc(T.sem.loaded, 16)
+    g.wait_ge(T.sem.loaded, 32)
 
     g.remote_dma_fused(
         [
             RemoteDMATransfer(
-                srcs=[T.xs[:, w - H:w]],
+                srcs=[T.edge[LAST]],
                 dsts=[T.halo[NORTH], T.halo[WEST]],
                 dst_ids=[dst_id(i + 1, j), dst_id(i, j + 1)],
                 dma_engine_mask=LOW,
                 remote_sem=T.sem.arrived,
             ),
             RemoteDMATransfer(
-                srcs=[T.xs[:, 0:H]],
+                srcs=[T.edge[FIRST]],
                 dsts=[T.halo[SOUTH], T.halo[EAST]],
                 dst_ids=[dst_id(i - 1, j), dst_id(i, j - 1)],
                 dma_engine_mask=HIGH,

from concourse.bass import DstId, RemoteDMATransfer

H = 8
ROWS, COLS = 2, 4

SCRATCH = {
    "edge": ("dram", [2, 128, H], "float32"),
    "halo": ("dram", [4, 128, H], "float32"),
}
SEMAPHORES = ["loaded", "read", "arrived", "stored"]

LOW, HIGH = 0x00FF, 0xFF00
LAST, FIRST = 0, 1
NORTH, SOUTH, WEST, EAST = 0, 1, 2, 3


def rank_program(g, core, T, topo):
    rank = T.rank_of(core)
    if rank is None:
        return
    i, j = divmod(rank, COLS)
    w = T.x.shape[1]

    def dst_id(a, b):
        rid, pid, sengine = topo.addr(T.cores[(a % ROWS) * COLS + (b % COLS)])
        return DstId(rid=rid, pnc=pid)

    g.dma_start(T.edge[LAST], T.x[:, w - H:w]).then_inc(T.sem.loaded, 16)
    g.dma_start(T.edge[FIRST], T.x[:, 0:H]).then_inc(T.sem.loaded, 16)
    g.wait_ge(T.sem.loaded, 32)

    g.remote_dma_fused(
        [
            RemoteDMATransfer(
                srcs=[T.edge[LAST]],
                dsts=[T.halo[NORTH], T.halo[WEST]],
                dst_ids=[dst_id(i + 1, j), dst_id(i, j + 1)],
                dma_engine_mask=LOW,
                remote_sem=T.sem.arrived,
            ),
            RemoteDMATransfer(
                srcs=[T.edge[FIRST]],
                dsts=[T.halo[SOUTH], T.halo[EAST]],
                dst_ids=[dst_id(i - 1, j), dst_id(i, j - 1)],
                dma_engine_mask=HIGH,
                remote_sem=T.sem.arrived,
            ),
        ],
        local_sem=T.sem.read,
    )

    g.wait_ge(T.sem.arrived, 32)
    g.dma_start(T.y[:], T.halo[:]).then_inc(T.sem.stored, 16)
    g.wait_ge(T.sem.stored, 16)
    g.wait_ge(T.sem.read, 16)
